import numpy as np
import ml_dtypes


def mxq(x, axis, fmt="e4m3"):
    dtype, down = {"e4m3": (ml_dtypes.float8_e4m3fn, 7), "e5m2": (ml_dtypes.float8_e5m2, 14)}[fmt]
    v = np.moveaxis(np.asarray(x, np.float32).astype(ml_dtypes.bfloat16).astype(np.float64), axis, -1)
    blocks = v.reshape(v.shape[:-1] + (-1, 32))
    amax = np.abs(blocks).max(-1, keepdims=True)
    byte = np.maximum(np.where(amax > 0, np.frexp(amax)[1] - 1 + 127, 0) - down, 1)
    scale = np.exp2(byte - 127.0)
    codes = (blocks / scale).astype(np.float32).astype(dtype).astype(np.float64)
    return np.moveaxis((codes * scale).reshape(v.shape), -1, axis)


WIDE = False


def mx_kscale(k):
    if not WIDE:
        return np.ones(k)
    levels = np.array([10, -10, 5, -5, 0])
    if k % 512:
        return np.exp2(np.random.permutation(np.resize(levels, k // 32))).repeat(32)
    a = np.empty((k // 512, 16))
    for p in range(k // 512):
        a[p, :8] = np.random.permutation(np.resize(levels, 8))
        for g in range(8):
            far = levels[np.abs(levels - a[p, g]) >= 10]
            a[p, g + 8] = far[np.random.randint(len(far))]
    return np.exp2(a.ravel()).repeat(32)


BF16 = ml_dtypes.bfloat16


def bf(x):
    return np.asarray(x, np.float32).astype(BF16)


def f64(x):
    return np.asarray(x).astype(np.float64)


E2M1 = np.array([0.0, 0.5, 1.0, 1.5, 2.0, 3.0, 4.0, 6.0, -0.0, -0.5, -1.0, -1.5, -2.0, -3.0, -4.0, -6.0])


def pack_weight(w, fmt):
    k, n = w.shape
    w = f64(bf(w)).reshape(k // 32, 32, n)
    amax = np.abs(w).max(1)
    if fmt == "e4m3":
        byte = np.frexp(amax)[1] - 1 + 127 - 7
    else:
        mant, ex = np.frexp(amax / 6.0)
        byte = np.where(mant > 0.5, ex, ex - 1) + 127
    byte = np.clip(np.where(amax > 0, byte, 1), 1, 254)
    scaled = (w * np.exp2(127.0 - byte)[:, None, :]).reshape(k, n).astype(np.float32)
    by_word = np.ascontiguousarray(scaled.reshape(k // 512, 128, 4, n).transpose(0, 1, 3, 2))
    if fmt == "e4m3":
        words = by_word.astype(ml_dtypes.float8_e4m3fn).view(np.uint8)
    else:
        c = by_word.astype(ml_dtypes.float4_e2m1fn).view(np.uint8) & 0xF
        words = c[..., 0::2] | (c[..., 1::2] << 4)
    return np.ascontiguousarray(words), np.ascontiguousarray(byte.astype(np.uint8).reshape(k // 512, 16, n))


def unpack_weight(words, scales, fmt):
    g, p, n, _ = words.shape
    if fmt == "e4m3":
        vals = np.ascontiguousarray(words).view(ml_dtypes.float8_e4m3fn).astype(np.float64)
    else:
        nib = np.empty((g, p, n, 4), np.uint8)
        nib[..., 0::2] = words & 0xF
        nib[..., 1::2] = words >> 4
        vals = E2M1[nib]
    vals = vals * np.repeat(np.exp2(scales.astype(np.float64) - 127.0), 8, axis=1)[..., None]
    return vals.transpose(0, 1, 3, 2).reshape(g * 512, n)
def pack4(w):
    words, scales = pack_weight(w, "e2m1")
    return words.reshape(words.shape[0], 128, -1), scales


def unpack4(words, scales):
    return unpack_weight(words.reshape(words.shape[0], 128, -1, 2), scales, "e2m1")


def planes(Y):
    n, m = Y.shape
    b = f64(bf(Y)).reshape(n // 32, 32, m)
    amax = np.abs(b).max(1)
    byte = np.clip(np.where(amax > 0, np.frexp(amax)[1] - 1 + 127 - 7, 1), 1, 254)
    codes = (b * np.exp2(127.0 - byte)[:, None, :]).reshape(n, m).astype(np.float32).astype(ml_dtypes.float8_e4m3fn).view(np.uint8)
    words = codes.reshape(n // 512, 128, 4, m).transpose(0, 1, 3, 2)
    return np.ascontiguousarray(words), np.ascontiguousarray(byte.astype(np.uint8).reshape(n // 512, 16, m))


T, C, F, D = 1024, 1024, 2048, 1024


def setup_inputs():
    s = mx_kscale(C)
    t = mx_kscale(T)
    E = np.random.randn(T, C) * t[:, None] * s[None, :]
    Wt = np.random.randn(C, F) / np.sqrt(C) / s[:, None]
    wt_words, wt_scales = pack4(Wt)
    Z = 1.5 * np.random.randn(T, F)
    X = 2.0 * np.random.randn(T, D) / np.sqrt(T) / t[:, None]
    rate = np.exp(0.8 * np.random.randn(F))
    precond = np.exp(0.3 * np.random.randn(D, F))
    return {"errors": bf(E), "wt_words": wt_words, "wt_scales": wt_scales,
            "preact": bf(Z), "x": bf(X), "rate": bf(rate), "precond": bf(precond)}


def reference(errors, wt_words, wt_scales, preact, x, rate, precond):
    E, Z, X = f64(errors), f64(preact), f64(x)
    Wt = unpack4(wt_words, wt_scales)
    back = mxq(E, 1, "e4m3") @ Wt
    delta = back * (1.0 / (1.0 + np.exp(-Z)))
    G = mxq(X, 0, "e4m3").T @ mxq(delta, 0, "e4m3")
    y = G * f64(rate)[None, :] * f64(precond)
    Y = y.T
    words, scales = planes(Y)
    return y, words, scales

@@ -1,0 +1,683 @@
+from contextlib import ExitStack
+
+import concourse.mybir as mybir
+from concourse.masks import make_identity
+
+T, C, F, D = 1024, 1024, 2048, 1024
+FLOPS = 2 * T * C * F + 2 * T * D * F
+
+F32 = mybir.dt.float32
+BF16 = mybir.dt.bfloat16
+I32 = mybir.dt.int32
+U32 = mybir.dt.uint32
+U8 = mybir.dt.uint8
+FP8X4 = mybir.dt.float8_e4m3fn_x4
+FP4X4 = mybir.dt.float4_e2m1fn_x4
+MULT = mybir.AluOpType.mult
+ADD = mybir.AluOpType.add
+SIGMOID = mybir.ActivationFunctionType.Sigmoid
+
+P = 128
+CHUNKS = 4
+
+
+def plan():
+    return [
+        ("load_rate",),
+        ("load_e", 0, 0),
+        ("load_e", 0, 1),
+        ("load_x", 0, 0),
+        ("load_x", 1, 0),
+        ("load_e", 1, 0),
+        ("load_e", 1, 1),
+        ("load_wsc", 0, 1),
+        ("load_w", 0, 1),
+        ("load_z", 0, 0),
+        ("load_z", 0, 1),
+        ("load_p", 0, 0),
+        ("load_x", 0, 1),
+        ("load_w", 1, 2),
+        ("load_wsc", 1, 4),
+        ("load_z", 1, 0),
+        ("load_x", 1, 1),
+        ("load_p", 0, 1),
+        ("load_z", 1, 1),
+        ("load_p", 1, 0),
+        ("load_p", 1, 1),
+        ("load_w", 2, 4),
+        ("load_z", 2, 0),
+        ("load_p", 2, 0),
+        ("load_z", 2, 1),
+        ("load_p", 2, 1),
+        ("load_z", 3, 0),
+        ("load_p", 3, 0),
+        ("load_z", 3, 1),
+        ("load_p", 3, 1),
+        ("rate_t", 0),
+        ("rate_t", 1),
+        ("rate_c", 0, "s"),
+        ("rate_c", 1, "s"),
+        ("e_t", 0, 0),
+        ("e_c", 0, 0, "s"),
+        ("e_t", 0, 1),
+        ("e_c", 0, 1, "s"),
+        ("e_t", 0, 2),
+        ("e_c", 0, 2, "s"),
+        ("e_t", 0, 3),
+        ("e_c", 0, 3, "s"),
+        ("x_i", 0, 0, 0, "v"),
+        ("x_i", 0, 0, 1, "v"),
+        ("e_q4", 0),
+        ("x_i", 1, 0, 0, "v"),
+        ("x_i", 1, 0, 1, "v"),
+        ("e_t", 1, 0),
+        ("e_c", 1, 0, "s"),
+        ("e_t", 1, 1),
+        ("e_c", 1, 1, "v"),
+        ("e_t", 1, 2),
+        ("e_c", 1, 2, "s"),
+        ("x_q", 0),
+        ("e_t", 1, 3),
+        ("e_c", 1, 3, "v"),
+        ("sig", 0, 0),
+        ("e_q4", 1),
+        ("sig", 0, 1),
+        ("sig", 0, 2),
+        ("sig", 0, 3),
+        ("m1", 0, 0),
+        ("d", 0, 0),
+        ("m1", 0, 1),
+        ("d", 0, 1),
+        ("m1", 0, 2),
+        ("d", 0, 2),
+        ("m1", 0, 3),
+        ("d", 0, 3),
+        ("m1", 0, 4),
+        ("d", 0, 4),
+        ("m1", 0, 5),
+        ("d", 0, 5),
+        ("m1", 0, 6),
+        ("d", 0, 6),
+        ("m1", 0, 7),
+        ("d", 0, 7),
+        ("x_i", 0, 1, 0, "s"),
+        ("x_i", 0, 1, 1, "s"),
+        ("sig", 1, 0),
+        ("d_q", 0),
+        ("x_i", 1, 1, 0, "s"),
+        ("sig", 1, 1),
+        ("x_i", 1, 1, 1, "s"),
+        ("m1", 1, 0),
+        ("d", 1, 0),
+        ("m1", 1, 1),
+        ("d", 1, 1),
+        ("rp", 0, 1, "g"),
+        ("rp", 0, 0, "g"),
+        ("rp", 0, 3, "g"),
+        ("rp", 0, 2, "g"),
+        ("rp", 0, 5, "g"),
+        ("rp", 0, 4, "g"),
+        ("rp", 0, 7, "g"),
+        ("rp", 0, 6, "g"),
+        ("rp", 1, 1, "g"),
+        ("rp", 1, 0, "g"),
+        ("rp", 1, 3, "g"),
+        ("rp", 1, 2, "g"),
+        ("rp", 1, 5, "g"),
+        ("rp", 1, 4, "g"),
+        ("rp", 1, 7, "g"),
+        ("rp", 1, 6, "g"),
+        ("rp", 2, 1, "g"),
+        ("rp", 2, 0, "g"),
+        ("rp", 2, 3, "g"),
+        ("rp", 2, 2, "g"),
+        ("rp", 2, 5, "g"),
+        ("rp", 2, 4, "g"),
+        ("rp", 2, 7, "g"),
+        ("rp", 2, 6, "g"),
+        ("rp", 3, 1, "g"),
+        ("rp", 3, 0, "g"),
+        ("rp", 3, 3, "g"),
+        ("rp", 3, 2, "g"),
+        ("rp", 3, 5, "g"),
+        ("rp", 3, 4, "g"),
+        ("rp", 3, 7, "g"),
+        ("rp", 3, 6, "g"),
+        ("m1", 1, 2),
+        ("d", 1, 2),
+        ("m1", 1, 3),
+        ("d", 1, 3),
+        ("sig", 1, 2),
+        ("sig", 1, 3),
+        ("sig", 2, 0),
+        ("m1", 1, 4),
+        ("m2", 0, 0),
+        ("y", 0, 0),
+        ("d", 1, 4),
+        ("sig", 2, 1),
+        ("m1", 1, 5),
+        ("m2", 0, 1),
+        ("y", 0, 1),
+        ("d", 1, 5),
+        ("x_q", 1),
+        ("cast2", 0, 0, "s"),
+        ("store_y", 0, 0),
+        ("m1", 1, 6),
+        ("m2", 0, 2),
+        ("y", 0, 2),
+        ("d", 1, 6),
+        ("sig", 2, 2),
+        ("m1", 1, 7),
+        ("m2", 0, 3),
+        ("y", 0, 3),
+        ("d", 1, 7),
+        ("cast2", 0, 1, "s"),
+        ("store_y", 0, 1),
+        ("m1", 2, 0),
+        ("m2", 0, 4),
+        ("y", 0, 4),
+        ("d", 2, 0),
+        ("d_q", 1),
+        ("sig", 2, 3),
+        ("m1", 2, 1),
+        ("m2", 0, 5),
+        ("y_t2", 0, 0),
+        ("y_t2", 0, 1),
+        ("y", 0, 5),
+        ("d", 2, 1),
+        ("cast2", 0, 2, "s"),
+        ("store_y", 0, 2),
+        ("y_c", 0, 0, "s"),
+        ("m1", 2, 2),
+        ("m2", 0, 6),
+        ("y", 0, 6),
+        ("d", 2, 2),
+        ("y_c", 0, 1, "s"),
+        ("sig", 3, 0),
+        ("m1", 2, 3),
+        ("m2", 0, 7),
+        ("y", 0, 7),
+        ("d", 2, 3),
+        ("cast2", 0, 3, "s"),
+        ("store_y", 0, 3),
+        ("m1", 2, 4),
+        ("m2", 1, 0),
+        ("y", 1, 0),
+        ("d", 2, 4),
+        ("sig", 3, 1),
+        ("m1", 2, 5),
+        ("m2", 1, 1),
+        ("y", 1, 1),
+        ("d", 2, 5),
+        ("cast2", 1, 0, "s"),
+        ("store_y", 1, 0),
+        ("m1", 2, 6),
+        ("m2", 1, 2),
+        ("y", 1, 2),
+        ("d", 2, 6),
+        ("sig", 3, 2),
+        ("m1", 2, 7),
+        ("m2", 1, 3),
+        ("y", 1, 3),
+        ("d", 2, 7),
+        ("cast2", 1, 1, "s"),
+        ("store_y", 1, 1),
+        ("m1", 3, 0),
+        ("m2", 1, 4),
+        ("y_t2", 0, 2),
+        ("y_t2", 0, 3),
+        ("y", 1, 4),
+        ("d", 3, 0),
+        ("y_c", 0, 2, "s"),
+        ("y_c", 0, 3, "s"),
+        ("d_q", 2),
+        ("sig", 3, 3),
+        ("m1", 3, 1),
+        ("m2", 1, 5),
+        ("y_t2", 1, 0),
+        ("y_t2", 1, 1),
+        ("y", 1, 5),
+        ("d", 3, 1),
+        ("cast2", 1, 2, "s"),
+        ("store_y", 1, 2),
+        ("y_c", 1, 0, "s"),
+        ("y_q", 0, 0, 4),
+        ("m1", 3, 2),
+        ("m2", 1, 6),
+        ("y", 1, 6),
+        ("d", 3, 2),
+        ("y_c", 1, 1, "s"),
+        ("m1", 3, 3),
+        ("m2", 1, 7),
+        ("y", 1, 7),
+        ("d", 3, 3),
+        ("cast2", 1, 3, "s"),
+        ("store_y", 1, 3),
+        ("store_codes", 0, 0, 4),
+        ("m1", 3, 4),
+        ("m2", 2, 0),
+        ("y", 2, 0),
+        ("d", 3, 4),
+        ("m1", 3, 5),
+        ("m2", 2, 1),
+        ("y", 2, 1),
+        ("d", 3, 5),
+        ("cast2", 2, 0, "s"),
+        ("store_y", 2, 0),
+        ("m1", 3, 6),
+        ("m2", 2, 2),
+        ("y", 2, 2),
+        ("d", 3, 6),
+        ("m1", 3, 7),
+        ("m2", 2, 3),
+        ("y", 2, 3),
+        ("d", 3, 7),
+        ("cast2", 2, 1, "s"),
+        ("store_y", 2, 1),
+        ("m2", 2, 4),
+        ("y_t2", 1, 2),
+        ("y_t2", 1, 3),
+        ("y", 2, 4),
+        ("y_c", 1, 2, "s"),
+        ("y_c", 1, 3, "s"),
+        ("d_q", 3),
+        ("m2", 2, 5),
+        ("y_t2", 2, 0),
+        ("y_t2", 2, 1),
+        ("y", 2, 5),
+        ("cast2", 2, 2, "s"),
+        ("store_y", 2, 2),
+        ("y_c", 2, 0, "s"),
+        ("y_q", 1, 0, 4),
+        ("m2", 2, 6),
+        ("y", 2, 6),
+        ("y_c", 2, 1, "s"),
+        ("m2", 2, 7),
+        ("y", 2, 7),
+        ("cast2", 2, 3, "s"),
+        ("store_y", 2, 3),
+        ("store_codes", 1, 0, 4),
+        ("m2", 3, 0),
+        ("y", 3, 0),
+        ("m2", 3, 1),
+        ("y", 3, 1),
+        ("cast2", 3, 0, "s"),
+        ("store_y", 3, 0),
+        ("m2", 3, 2),
+        ("y_t2", 2, 2),
+        ("y_t2", 2, 3),
+        ("y", 3, 2),
+        ("y_c", 2, 2, "s"),
+        ("y_c", 2, 3, "s"),
+        ("m2", 3, 3),
+        ("y", 3, 3),
+        ("cast2", 3, 1, "s"),
+        ("store_y", 3, 1),
+        ("m2", 3, 4),
+        ("y", 3, 4),
+        ("m2", 3, 5),
+        ("y_t2", 3, 0),
+        ("y", 3, 5),
+        ("cast2", 3, 2, "s"),
+        ("store_y", 3, 2),
+        ("y_c", 3, 0, "s"),
+        ("y_q", 2, 0, 4),
+        ("store_codes", 2, 0, 4),
+        ("store_scales", 0, 3),
+        ("m2", 3, 6),
+        ("y", 3, 6),
+        ("cast1", 3, 6, "s"),
+        ("store_y1", 3, 6),
+        ("m2", 3, 7),
+        ("y_t2", 3, 1),
+        ("y_t2", 3, 2),
+        ("y", 3, 7),
+        ("cast1", 3, 7, "v"),
+        ("store_y1", 3, 7),
+        ("y_c", 3, 1, "s"),
+        ("y_c", 3, 2, "v"),
+        ("y_q", 3, 0, 2),
+        ("store_codes", 3, 0, 2),
+        ("y_q", 3, 2, 3),
+        ("store_codes", 3, 2, 3),
+        ("y_t1", 3, 6),
+        ("y_c1", 3, 6, "s"),
+        ("y_t1", 3, 7),
+        ("y_c1", 3, 7, "s"),
+        ("y_q", 3, 3, 4),
+        ("store_codes", 3, 3, 4),
+        ("store_scales", 3, 4),
+    ]
+
+
+def tile_preconditioned_softplus_gradient_h1_kernel(
+    tc, errors, wt_words, wt_scales, preact, x, rate, precond, out_0, out_1, out_2
+):
+    nc = tc.nc
+    with ExitStack() as ctx:
+        sb = ctx.enter_context(tc.tile_pool(name="sb", bufs=1))
+        psum = ctx.enter_context(tc.psum_pool(name="psum", bufs=1))
+        ctx.enter_context(tc.manual_schedule())
+        live = {}
+
+        def ring(key, tag, bufs, shape, dtype):
+            if key not in live:
+                live[key] = sb.tile(shape, dtype, name=tag, tag=tag, bufs=bufs, align_bytes=64)
+            return live[key]
+
+        def bank(key, tag, bufs):
+            live[key] = psum.tile([P, 512], F32, name=tag, tag=tag, bufs=bufs)
+            return live[key]
+
+        def copy(eng, out, in_):
+            if eng == "v":
+                nc.vector.tensor_copy(out=out, in_=in_)
+            elif eng == "s":
+                nc.scalar.copy(out=out, in_=in_)
+            else:
+                nc.gpsimd.tensor_scalar(out=out, in0=in_, scalar1=1.0, scalar2=-0.0, op0=MULT, op1=ADD)
+
+        ident = sb.tile([P, P], F32, name="ident")
+        warm = sb.tile([P, 8], F32, name="warm")
+        warm2 = sb.tile([P, 8], F32, name="warm2")
+        rate_words = sb.tile([P, 16], BF16, name="rate_words")
+        rate_all = sb.tile([P, F], BF16, name="rate_all")
+        w_scales = {}
+        for lo, hi in ((0, 1), (1, 4)):
+            plane = sb.tile([P, 2, 512 * (hi - lo)], U8, name="w_scales_%d" % lo, align_bytes=64)
+            for c in range(lo, hi):
+                w_scales[c] = (plane, lo)
+        w_words = {}
+        for lo, hi in ((0, 1), (1, 2), (2, 4)):
+            words = sb.tile([P, 2, 1024 * (hi - lo)], U8, name="w_words_%d" % lo, align_bytes=64)
+            for c in range(lo, hi):
+                w_words[c] = (words, lo)
+        e_codes = sb.tile([P, 2, 1024], U32, name="e_codes", align_bytes=64)
+        e_scales = sb.tile([P, 2, 1024], U8, name="e_scales", align_bytes=64)
+        x_codes = sb.tile([P, 2, 1024], U32, name="x_codes", align_bytes=64)
+        x_scales = sb.tile([P, 2, 1024], U8, name="x_scales", align_bytes=64)
+        y_scales = sb.tile([P, CHUNKS, D], U8, name="y_scales", align_bytes=64)
+
+        for c in (0, 1):
+            nc.vector.memset(w_scales[c][0][:].rearrange("p g n -> p (g n)").bitcast(I32), 0)
+        nc.vector.memset(warm[:], 0.0)
+        nc.scalar.activation(out=warm2[:], in_=warm[:], func=SIGMOID)
+        make_identity(nc, ident[:])
+
+        def raw(key, shape):
+            return ring(key, "raw", 16, shape, BF16)
+
+        def load_rate():
+            nc.sync.dma_start(out=rate_words[:], in_=rate.rearrange("(p m) -> p m", p=P))
+
+        def load_e(g, h):
+            rows = errors[512 * g : 512 * (g + 1), :].rearrange("(m t) k -> m t k", t=4)
+            nc.sync.dma_start(out=raw(("e", g, h), [P, 2, C])[:], in_=rows[:, 2 * h : 2 * h + 2, :])
+
+        def load_wsc(lo, hi):
+            cols = slice(512 * lo, 512 * hi)
+            for q in range(4):
+                nc.sync.dma_start(
+                    out=w_scales[lo][0][32 * q : 32 * q + 4, :, :].bitcast(I32),
+                    in_=wt_scales[:, 4 * q : 4 * q + 4, cols].rearrange("g r n -> r g n").bitcast(I32),
+                )
+
+        def load_w(lo, hi):
+            cols = slice(1024 * lo, 1024 * hi)
+            words = wt_words.rearrange("g p n -> p g n")
+            nc.sync.dma_start(out=w_words[lo][0][:].bitcast(I32), in_=words[:, :, cols].bitcast(I32))
+
+        def load_z(c, g):
+            rows = preact[512 * g : 512 * (g + 1), 512 * c : 512 * (c + 1)]
+            nc.sync.dma_start(out=raw(("z", c, g), [P, 4, 512])[:], in_=rows.rearrange("(p t) f -> p t f", t=4))
+
+        def load_p(c, h):
+            rows = precond[512 * h : 512 * (h + 1), 512 * c : 512 * (c + 1)]
+            nc.sync.dma_start(out=raw(("p", c, h), [P, 4, 512])[:], in_=rows.rearrange("(a p) f -> p a f", p=P))
+
+        def load_x(g, dh):
+            rows = x[512 * g : 512 * (g + 1), 512 * dh : 512 * (dh + 1)]
+            nc.sync.dma_start(out=raw(("x", g, dh), [P, 4, 512])[:], in_=rows.rearrange("(p t) d -> p t d", t=4))
+
+        def rate_t(h):
+            b = bank(("rate", h), "m2", 3)
+            words = rate_words[:].bitcast(F32)
+            for m in range(4):
+                col = words[:, 4 * h + m : 4 * h + m + 1].to_broadcast([P, P])
+                nc.tensor.transpose(b[:, P * m : P * (m + 1)], col, ident[:])
+
+        def rate_c(h, eng):
+            out = rate_all[:].bitcast(F32).rearrange("p (n m) -> p n m", m=8)[:, :, 4 * h : 4 * h + 4]
+            copy(eng, out, live[("rate", h)][:].rearrange("p (m n) -> p n m", m=4))
+
+        def rp(c, j, eng):
+            ry = ring(("ry", c, j // 2), "ry", 13, [P, 2, 512], F32)
+            engine = nc.gpsimd if eng == "g" else nc.vector
+            engine.tensor_tensor(
+                out=ry[:, j % 2, :],
+                in0=live[("p", c, j // 4)][:, j % 4, :],
+                in1=rate_all[:, 512 * c : 512 * (c + 1)],
+                op=MULT,
+            )
+
+        def rp2(c, jj, eng):
+            ry = ring(("ry", c, jj), "ry", 13, [P, 2, 512], F32)
+            engine = nc.gpsimd if eng == "g" else nc.vector
+            row = rate_all[:, 512 * c : 512 * (c + 1)].rearrange("p (a f) -> p a f", a=1)
+            engine.tensor_tensor(
+                out=ry[:],
+                in0=live[("p", c, jj // 2)][:, 2 * (jj % 2) : 2 * (jj % 2) + 2, :],
+                in1=row.to_broadcast([P, 2, 512]),
+                op=MULT,
+            )
+
+        def e_q4(g):
+            nc.vector.quantize_mx(
+                out=e_codes[:, g, :].bitcast(FP8X4), scales=e_scales[:, g, :], in_=live[("eT", g)][:]
+            )
+
+        def cast2(c, jj, eng):
+            yb = ring(("yb2", c, jj), "yb2", 4, [P, 1024], BF16)
+            copy(
+                eng,
+                yb[:].rearrange("p (a u m e) -> p a u m e", a=2, u=2, e=2),
+                live[("ry", c, jj)][:].rearrange("p a (m u e) -> p a u m e", u=2, e=2),
+            )
+
+        def y_t2(c, jj):
+            b = bank(("yt", c, jj), "tr", 2)
+            words = live[("yb2", c, jj)][:].bitcast(F32)
+            for i in range(4):
+                nc.tensor.transpose(b[:, P * i : P * (i + 1)], words[:, P * i : P * (i + 1)], ident[:])
+
+        def cast1(c, j, eng):
+            yb = ring(("yb2", c, j // 2), "yb2", 4, [P, 1024], BF16)[:, 512 * (j % 2) : 512 * (j % 2 + 1)]
+            copy(
+                eng,
+                yb.rearrange("p (u m e) -> p u m e", u=2, e=2),
+                live[("ry", c, j // 2)][:, j % 2, :].rearrange("p (m u e) -> p u m e", u=2, e=2),
+            )
+
+        def y_t1(c, j):
+            b = bank(("yth", c, j), "tr", 2)
+            words = live[("yb2", c, j // 2)][:].bitcast(F32)
+            for u in range(2):
+                i = 2 * (j % 2) + u
+                nc.tensor.transpose(b[:, P * u : P * (u + 1)], words[:, P * i : P * (i + 1)], ident[:])
+
+        def y_c1(c, j, eng):
+            dst = ring(("yT", c), "qb", 2, [P, 4096], BF16)[:].bitcast(F32)[:, 256 * j : 256 * (j + 1)]
+            copy(
+                eng,
+                dst.rearrange("p (d u) -> p d u", u=2),
+                live[("yth", c, j)][:, 0:256].rearrange("p (u d) -> p d u", u=2),
+            )
+
+        def store_y1(c, j):
+            rows = out_0[P * j : P * (j + 1), 512 * c : 512 * (c + 1)]
+            nc.sync.dma_start(out=rows, in_=live[("ry", c, j // 2)][:, j % 2, :])
+
+        def e_t(g, t):
+            b = bank(("et", g, t), "tr", 2) if t % 2 == 0 else bank(("et", g, t), "m2", 3)
+            words = live[("e", g, t // 2)][:].bitcast(F32)
+            for c in range(2):
+                for u in range(2):
+                    i = 2 * c + u
+                    nc.tensor.transpose(
+                        b[:, P * i : P * (i + 1)], words[:, t % 2, 256 * c + u : 256 * (c + 1) : 2], ident[:]
+                    )
+
+        def e_c(g, t, eng):
+            dst = ring(("eT", g), "qa" if g == 0 else "qb", 2, [P, 4096], BF16)[:].bitcast(F32)[:, 512 * t : 512 * (t + 1)]
+            copy(
+                eng,
+                dst.rearrange("p (c m u) -> p c m u", c=2, u=2),
+                live[("et", g, t)][:].rearrange("p (c u m) -> p c m u", c=2, u=2),
+            )
+
+        def e_q(g, h):
+            cols = slice(512 * h, 512 * (h + 1))
+            nc.vector.quantize_mx(
+                out=e_codes[:, g, cols].bitcast(FP8X4),
+                scales=e_scales[:, g, cols],
+                in_=live[("eT", g)][:, 2048 * h : 2048 * (h + 1)],
+            )
+
+        def sig(c, i):
+            g, h = divmod(i, 2)
+            out = ring(("sig", c, i), "sig", 4, [P, 1024], F32)
+            z = live[("z", c, g)][:, :, 256 * h : 256 * (h + 1)]
+            nc.scalar.activation(
+                out=out[:].rearrange("p (u f e) -> p u f e", u=2, e=2),
+                in_=z.rearrange("p (u e) f -> p u f e", u=2),
+                func=SIGMOID,
+            )
+
+        def m1(c, k):
+            g, s = divmod(k, 4)
+            b = bank(("m1", c, k), "m1", 3)
+            words, w0 = w_words[c]
+            plane, s0 = w_scales[c]
+            w0 = 2 * (512 * (c - w0) + P * s)
+            s0 = 512 * (c - s0) + P * s
+            for t in range(4):
+                for h in range(2):
+                    cols = slice(256 * t + P * h, 256 * t + P * (h + 1))
+                    w = words[:, h, w0 : w0 + 256]
+                    nc.tensor.matmul_mx(
+                        out=b[:, P * t : P * (t + 1)],
+                        lhsT=e_codes[:, g, cols].bitcast(FP8X4),
+                        lhsT_scale=e_scales[:, g, cols],
+                        rhs=w.bitcast(FP4X4),
+                        rhs_scale=plane[:, h, s0 : s0 + P],
+                        start=(h == 0),
+                        stop=(h == 1),
+                    )
+
+        def d(c, k):
+            g, s = divmod(k, 4)
+            dl = ring(("dl", c), "qa", 2, [P, 4096], BF16)
+            gate = live[("sig", c, k // 2)][:].rearrange("p (u f e) -> p f u e", u=2, e=2)
+            nc.vector.tensor_tensor(
+                out=dl[:, 512 * k : 512 * (k + 1)].rearrange("p (f u e) -> p f u e", u=2, e=2),
+                in0=live[("m1", c, k)][:].rearrange("p (u e f) -> p f u e", u=2, e=2),
+                in1=gate[:, P * (k % 2) : P * (k % 2 + 1), :, :],
+                op=MULT,
+            )
+
+        def d_q(c):
+            codes = ring(("dc", c), "d_codes", 2, [P, 1024], U32)
+            scales = ring(("ds", c), "d_scales", 2, [P, 1024], U8)
+            nc.vector.quantize_mx(out=codes[:].bitcast(FP8X4), scales=scales[:], in_=live[("dl", c)][:])
+
+        def x_i(g, dh, q, eng):
+            dst = ring(("xi", dh), "qb", 2, [P, 4096], BF16)[:, 2048 * g + 1024 * q : 2048 * g + 1024 * (q + 1)]
+            src = live[("x", g, dh)][:, :, 256 * q : 256 * (q + 1)]
+            copy(
+                eng,
+                dst.rearrange("p (c i t) -> p c t i", i=4, t=4),
+                src.rearrange("p t (c i) -> p c t i", i=4),
+            )
+
+        def x_q(dh):
+            nc.vector.quantize_mx(
+                out=x_codes[:, dh, :].bitcast(FP8X4), scales=x_scales[:, dh, :], in_=live[("xi", dh)][:]
+            )
+
+        def m2(c, j):
+            b = bank(("m2", c, j), "m2", 3)
+            dh, a = divmod(j, 4)
+            for g in range(2):
+                cols = slice(512 * g + P * a, 512 * g + P * (a + 1))
+                nc.tensor.matmul_mx(
+                    out=b[:],
+                    lhsT=x_codes[:, dh, cols].bitcast(FP8X4),
+                    lhsT_scale=x_scales[:, dh, cols],
+                    rhs=live[("dc", c)][:, 512 * g : 512 * (g + 1)].bitcast(FP8X4),
+                    rhs_scale=live[("ds", c)][:, 512 * g : 512 * (g + 1)],
+                    start=(g == 0),
+                    stop=(g == 1),
+                )
+
+        def y(c, j):
+            ry = live[("ry", c, j // 2)][:, j % 2, :]
+            nc.vector.tensor_tensor(out=ry, in0=live[("m2", c, j)][:], in1=ry, op=MULT)
+
+        def cast(c, j, eng):
+            yb = ring(("yb", c, j), "yb", 8, [P, 512], BF16)
+            copy(
+                eng,
+                yb[:].rearrange("p (u m e) -> p u m e", u=2, e=2),
+                live[("ry", c, j // 2)][:, j % 2, :].rearrange("p (m u e) -> p u m e", u=2, e=2),
+            )
+
+        def y_t(c, jj):
+            b = bank(("yt", c, jj), "tr", 2)
+            for a in range(2):
+                words = live[("yb", c, 2 * jj + a)][:].bitcast(F32)
+                for u in range(2):
+                    i = 2 * a + u
+                    nc.tensor.transpose(b[:, P * i : P * (i + 1)], words[:, P * u : P * (u + 1)], ident[:])
+
+        def y_c(c, jj, eng):
+            dst = ring(("yT", c), "qb", 2, [P, 4096], BF16)[:].bitcast(F32)[:, 512 * jj : 512 * (jj + 1)]
+            copy(
+                eng,
+                dst.rearrange("p (a d u) -> p a d u", a=2, u=2),
+                live[("yt", c, jj)][:].rearrange("p (a u d) -> p a d u", a=2, u=2),
+            )
+
+        def y_q(c, lo, hi):
+            codes = ring(("yc", c), "y_codes", 2, [P, D], U32)
+            cols = slice(256 * lo, 256 * hi)
+            nc.vector.quantize_mx(
+                out=codes[:, cols].bitcast(FP8X4),
+                scales=y_scales[:, c, cols],
+                in_=live[("yT", c)][:, 1024 * lo : 1024 * hi],
+            )
+
+        def store_y(c, jj):
+            rows = out_0[256 * jj : 256 * (jj + 1), 512 * c : 512 * (c + 1)]
+            nc.sync.dma_start(out=rows.rearrange("(a p) f -> p a f", p=P), in_=live[("ry", c, jj)][:])
+
+        def store_codes(c, lo, hi):
+            cols = slice(256 * lo, 256 * hi)
+            words = out_1[c].rearrange("p m t -> p (m t)").bitcast(I32)
+            nc.sync.dma_start(out=words[:, cols], in_=live[("yc", c)][:, cols].bitcast(I32))
+
+        def store_scales(lo, hi):
+            for q in range(4):
+                nc.sync.dma_start(
+                    out=out_2[lo:hi, 4 * q : 4 * q + 4, :].rearrange("g r m -> r g m").bitcast(I32),
+                    in_=y_scales[32 * q : 32 * q + 4, lo:hi, :].bitcast(I32),
+                )
+
+        steps = {
+            "load_rate": load_rate, "load_e": load_e, "load_wsc": load_wsc, "load_w": load_w, "load_z": load_z,
+            "load_p": load_p, "load_x": load_x, "rate_t": rate_t, "rate_c": rate_c, "rp": rp, "cast1": cast1, "y_t1": y_t1, "y_c1": y_c1, "store_y1": store_y1, "rp2": rp2, "e_q4": e_q4, "cast2": cast2, "y_t2": y_t2, "e_t": e_t,
+            "e_c": e_c, "e_q": e_q, "sig": sig, "m1": m1, "d": d, "d_q": d_q, "x_i": x_i, "x_q": x_q, "m2": m2,
+            "y": y, "cast": cast, "y_t": y_t, "y_c": y_c, "y_q": y_q, "store_y": store_y,
+            "store_codes": store_codes, "store_scales": store_scales,
+        }
+        for step in plan():
+            steps[step[0]](*step[1:])

@@ -580,8 +580,8 @@ def tile_preconditioned_softplus_gradient_h1_kernel(
             gate = live[("sig", c, k // 2)][:].rearrange("p (u f e) -> p f u e", u=2, e=2)
             nc.vector.tensor_tensor(
                 out=dl[:, 512 * k : 512 * (k + 1)].rearrange("p (f u e) -> p f u e", u=2, e=2),
-                in0=live[("m1", c, k)][:].rearrange("p (u e f) -> p f u e", u=2, e=2),
-                in1=gate[:, P * (k % 2) : P * (k % 2 + 1), :, :],
+                in0=gate[:, P * (k % 2) : P * (k % 2 + 1), :, :],
+                in1=live[("m1", c, k)][:].rearrange("p (u e f) -> p f u e", u=2, e=2),
                 op=MULT,
             )
 
@@ -621,7 +621,7 @@ def tile_preconditioned_softplus_gradient_h1_kernel(
 
         def y(c, j):
             ry = live[("ry", c, j // 2)][:, j % 2, :]
-            nc.vector.tensor_tensor(out=ry, in0=live[("m2", c, j)][:], in1=ry, op=MULT)
+            nc.vector.tensor_tensor(out=ry, in0=ry, in1=live[("m2", c, j)][:], op=MULT)
 
         def cast(c, j, eng):
             yb = ring(("yb", c, j), "yb", 8, [P, 512], BF16)

@@ -17,333 +17,349 @@ MULT = mybir.AluOpType.mult
 ADD = mybir.AluOpType.add
 SIGMOID = mybir.ActivationFunctionType.Sigmoid
 
+COPY = mybir.ActivationFunctionType.Copy
+
 P = 128
+M1_BANKS, M2_BANKS, TR_BANKS = 2, 3, 3
+RY = 10
 CHUNKS = 4
 
 
 def plan():
     return [
-        ("load_rate",),
         ("load_e", 0, 0),
         ("load_e", 0, 1),
+        ("load_rate",),
         ("load_x", 0, 0),
-        ("load_x", 1, 0),
         ("load_e", 1, 0),
-        ("load_e", 1, 1),
         ("load_wsc", 0, 1),
+        ("load_x", 1, 0),
         ("load_w", 0, 1),
         ("load_z", 0, 0),
+        ("load_e", 1, 1),
+        ("load_rrows",),
         ("load_z", 0, 1),
-        ("load_p", 0, 0),
-        ("load_x", 0, 1),
         ("load_w", 1, 2),
         ("load_wsc", 1, 4),
         ("load_z", 1, 0),
+        ("load_p", 0, 0),
+        ("load_x", 0, 1),
+        ("load_w", 2, 4),
         ("load_x", 1, 1),
         ("load_p", 0, 1),
-        ("load_z", 1, 1),
         ("load_p", 1, 0),
-        ("load_p", 1, 1),
-        ("load_w", 2, 4),
+        ("load_z", 1, 1),
         ("load_z", 2, 0),
-        ("load_p", 2, 0),
+        ("load_p", 1, 1),
         ("load_z", 2, 1),
-        ("load_p", 2, 1),
         ("load_z", 3, 0),
-        ("load_p", 3, 0),
+        ("load_p", 2, 0),
         ("load_z", 3, 1),
+        ("load_p", 2, 1),
+        ("load_p", 3, 0),
         ("load_p", 3, 1),
-        ("rate_t", 0),
-        ("rate_t", 1),
-        ("rate_c", 0, "s"),
-        ("rate_c", 1, "s"),
         ("e_t", 0, 0),
-        ("e_c", 0, 0, "s"),
+        ("e_c", 0, 0, "v"),
         ("e_t", 0, 1),
         ("e_c", 0, 1, "s"),
-        ("e_t", 0, 2),
-        ("e_c", 0, 2, "s"),
-        ("e_t", 0, 3),
-        ("e_c", 0, 3, "s"),
         ("x_i", 0, 0, 0, "v"),
+        ("e_t", 0, 2),
+        ("e_t", 0, 3),
+        ("e_t", 1, 0),
+        ("e_c", 0, 2, "s"),
+        ("e_c", 0, 3, "s"),
+        ("rate_t", 0),
+        ("e_t", 1, 1),
         ("x_i", 0, 0, 1, "v"),
         ("e_q4", 0),
+        ("m1", 0, 0),
+        ("rate_c", 0, "s"),
+        ("e_c", 1, 0, "s"),
+        ("e_t", 1, 2),
+        ("e_c", 1, 1, "s"),
+        ("e_t", 1, 3),
+        ("m1", 0, 1),
+        ("sig", 0, 0),
         ("x_i", 1, 0, 0, "v"),
         ("x_i", 1, 0, 1, "v"),
-        ("e_t", 1, 0),
-        ("e_c", 1, 0, "s"),
-        ("e_t", 1, 1),
-        ("e_c", 1, 1, "v"),
-        ("e_t", 1, 2),
-        ("e_c", 1, 2, "s"),
-        ("x_q", 0),
-        ("e_t", 1, 3),
-        ("e_c", 1, 3, "v"),
-        ("sig", 0, 0),
-        ("e_q4", 1),
-        ("sig", 0, 1),
-        ("sig", 0, 2),
-        ("sig", 0, 3),
-        ("m1", 0, 0),
-        ("d", 0, 0),
-        ("m1", 0, 1),
-        ("d", 0, 1),
+        ("rate_t", 1),
         ("m1", 0, 2),
-        ("d", 0, 2),
+        ("sig", 0, 1),
+        ("e_c", 1, 2, "s"),
+        ("sig", 0, 2),
         ("m1", 0, 3),
-        ("d", 0, 3),
+        ("x_q", 0),
+        ("sig", 0, 3),
+        ("rcol_cast",),
+        ("d", 0, 0),
+        ("e_c", 1, 3, "v"),
+        ("d", 0, 1),
+        ("e_q4", 1),
+        ("d", 0, 2),
         ("m1", 0, 4),
-        ("d", 0, 4),
         ("m1", 0, 5),
-        ("d", 0, 5),
-        ("m1", 0, 6),
-        ("d", 0, 6),
-        ("m1", 0, 7),
-        ("d", 0, 7),
-        ("x_i", 0, 1, 0, "s"),
-        ("x_i", 0, 1, 1, "s"),
+        ("rate_c", 1, "s"),
+        ("d", 0, 3),
         ("sig", 1, 0),
-        ("d_q", 0),
+        ("rcol_t",),
+        ("m1", 0, 6),
+        ("x_i", 0, 1, 0, "s"),
+        ("m1", 0, 7),
+        ("d", 0, 4),
+        ("x_i", 0, 1, 1, "s"),
+        ("d", 0, 5),
+        ("rp2", 0, 0, "v"),
+        ("d", 0, 6),
         ("x_i", 1, 1, 0, "s"),
-        ("sig", 1, 1),
-        ("x_i", 1, 1, 1, "s"),
+        ("d", 0, 7),
+        ("rp2", 0, 1, "v"),
         ("m1", 1, 0),
         ("d", 1, 0),
         ("m1", 1, 1),
-        ("d", 1, 1),
-        ("rp", 0, 1, "g"),
-        ("rp", 0, 0, "g"),
-        ("rp", 0, 3, "g"),
-        ("rp", 0, 2, "g"),
-        ("rp", 0, 5, "g"),
-        ("rp", 0, 4, "g"),
-        ("rp", 0, 7, "g"),
-        ("rp", 0, 6, "g"),
-        ("rp", 1, 1, "g"),
-        ("rp", 1, 0, "g"),
-        ("rp", 1, 3, "g"),
-        ("rp", 1, 2, "g"),
-        ("rp", 1, 5, "g"),
-        ("rp", 1, 4, "g"),
-        ("rp", 1, 7, "g"),
-        ("rp", 1, 6, "g"),
-        ("rp", 2, 1, "g"),
-        ("rp", 2, 0, "g"),
-        ("rp", 2, 3, "g"),
-        ("rp", 2, 2, "g"),
-        ("rp", 2, 5, "g"),
-        ("rp", 2, 4, "g"),
-        ("rp", 2, 7, "g"),
-        ("rp", 2, 6, "g"),
-        ("rp", 3, 1, "g"),
-        ("rp", 3, 0, "g"),
-        ("rp", 3, 3, "g"),
-        ("rp", 3, 2, "g"),
-        ("rp", 3, 5, "g"),
-        ("rp", 3, 4, "g"),
-        ("rp", 3, 7, "g"),
-        ("rp", 3, 6, "g"),
         ("m1", 1, 2),
-        ("d", 1, 2),
+        ("d", 1, 1),
+        ("d_q", 0),
         ("m1", 1, 3),
+        ("x_i", 1, 1, 1, "s"),
+        ("x_q", 1),
+        ("sig", 1, 1),
+        ("m2", 0, 0),
+        ("m2c", 0, 1, 0),
+        ("m1", 1, 4),
+        ("m2", 0, 1),
+        ("m1", 1, 5),
+        ("m2c", 0, 1, 1),
+        ("d", 1, 2),
+        ("y", 0, 0),
+        ("m2", 0, 2),
+        ("m1", 1, 6),
         ("d", 1, 3),
         ("sig", 1, 2),
         ("sig", 1, 3),
-        ("sig", 2, 0),
-        ("m1", 1, 4),
-        ("m2", 0, 0),
-        ("y", 0, 0),
-        ("d", 1, 4),
-        ("sig", 2, 1),
-        ("m1", 1, 5),
-        ("m2", 0, 1),
-        ("y", 0, 1),
-        ("d", 1, 5),
-        ("x_q", 1),
-        ("cast2", 0, 0, "s"),
-        ("store_y", 0, 0),
-        ("m1", 1, 6),
-        ("m2", 0, 2),
-        ("y", 0, 2),
-        ("d", 1, 6),
-        ("sig", 2, 2),
         ("m1", 1, 7),
+        ("d", 1, 4),
+        ("rp2", 1, 0, "v"),
         ("m2", 0, 3),
-        ("y", 0, 3),
-        ("d", 1, 7),
-        ("cast2", 0, 1, "s"),
-        ("store_y", 0, 1),
+        ("m2c", 0, 1, 2),
+        ("d", 1, 5),
         ("m1", 2, 0),
-        ("m2", 0, 4),
-        ("y", 0, 4),
-        ("d", 2, 0),
-        ("d_q", 1),
-        ("sig", 2, 3),
         ("m1", 2, 1),
-        ("m2", 0, 5),
-        ("y_t2", 0, 0),
-        ("y_t2", 0, 1),
-        ("y", 0, 5),
-        ("d", 2, 1),
-        ("cast2", 0, 2, "s"),
-        ("store_y", 0, 2),
-        ("y_c", 0, 0, "s"),
+        ("m2c", 0, 1, 3),
+        ("rcol_c", "s"),
         ("m1", 2, 2),
-        ("m2", 0, 6),
-        ("y", 0, 6),
-        ("d", 2, 2),
-        ("y_c", 0, 1, "s"),
-        ("sig", 3, 0),
+        ("ev", 0, 1, 0, "s"),
+        ("sig", 2, 0),
+        ("y", 0, 1),
+        ("store_y", 0, 0),
+        ("sig", 2, 1),
+        ("ev", 0, 1, 1, "s"),
+        ("d", 1, 6),
+        ("cast2", 0, 0, "s"),
+        ("sig", 2, 2),
+        ("ev", 0, 1, 2, "s"),
+        ("d", 1, 7),
+        ("y", 0, 2),
+        ("d_q", 1),
+        ("d", 2, 0),
         ("m1", 2, 3),
-        ("m2", 0, 7),
-        ("y", 0, 7),
-        ("d", 2, 3),
-        ("cast2", 0, 3, "s"),
-        ("store_y", 0, 3),
-        ("m1", 2, 4),
+        ("m2c", 1, 1, 0),
         ("m2", 1, 0),
-        ("y", 1, 0),
-        ("d", 2, 4),
-        ("sig", 3, 1),
+        ("sig", 2, 3),
+        ("ev", 0, 1, 3, "s"),
+        ("m2c", 1, 1, 1),
+        ("d", 2, 1),
+        ("m1", 2, 4),
+        ("y", 0, 3),
+        ("store_y", 0, 1),
+        ("t1", 0, 4),
+        ("y_t2", 0, 0),
+        ("d", 2, 2),
+        ("rp2", 1, 1, "v"),
+        ("t1", 0, 5),
         ("m1", 2, 5),
-        ("m2", 1, 1),
-        ("y", 1, 1),
-        ("d", 2, 5),
-        ("cast2", 1, 0, "s"),
-        ("store_y", 1, 0),
+        ("m2c", 1, 1, 2),
         ("m1", 2, 6),
-        ("m2", 1, 2),
-        ("y", 1, 2),
-        ("d", 2, 6),
-        ("sig", 3, 2),
+        ("rp2", 2, 0, "v"),
+        ("d", 2, 3),
+        ("cast2", 0, 1, "s"),
+        ("ev", 1, 1, 0, "s"),
+        ("ev", 1, 1, 1, "s"),
+        ("sig", 3, 0),
+        ("y_c", 0, 0, "s"),
+        ("sig", 3, 1),
+        ("yc", 0, 4),
+        ("d", 2, 4),
+        ("y", 1, 0),
+        ("d", 2, 5),
+        ("yc", 0, 5),
+        ("store_y", 0, 2),
+        ("rp2", 2, 1, "v"),
+        ("m2c", 1, 1, 3),
+        ("t1", 0, 6),
+        ("y_t2", 0, 1),
+        ("t1", 0, 7),
         ("m1", 2, 7),
-        ("m2", 1, 3),
-        ("y", 1, 3),
+        ("m2", 1, 1),
+        ("yc", 0, 6),
+        ("d", 2, 6),
         ("d", 2, 7),
-        ("cast2", 1, 1, "s"),
-        ("store_y", 1, 1),
+        ("ev", 1, 1, 2, "s"),
+        ("cast2", 0, 2, "s"),
+        ("ev", 1, 1, 3, "s"),
+        ("sig", 3, 2),
+        ("y_c", 0, 1, "s"),
+        ("yc", 0, 7),
+        ("store_y", 0, 3),
+        ("m2", 1, 2),
+        ("m2", 1, 3),
         ("m1", 3, 0),
-        ("m2", 1, 4),
-        ("y_t2", 0, 2),
-        ("y_t2", 0, 3),
-        ("y", 1, 4),
-        ("d", 3, 0),
-        ("y_c", 0, 2, "s"),
-        ("y_c", 0, 3, "s"),
+        ("t1", 1, 4),
         ("d_q", 2),
-        ("sig", 3, 3),
+        ("d", 3, 0),
+        ("t1", 1, 5),
+        ("y", 1, 1),
+        ("store_y", 1, 0),
         ("m1", 3, 1),
-        ("m2", 1, 5),
-        ("y_t2", 1, 0),
-        ("y_t2", 1, 1),
-        ("y", 1, 5),
-        ("d", 3, 1),
-        ("cast2", 1, 2, "s"),
-        ("store_y", 1, 2),
-        ("y_c", 1, 0, "s"),
-        ("y_q", 0, 0, 4),
+        ("cast2", 0, 3, "s"),
+        ("yc", 1, 4),
+        ("m2c", 2, 1, 0),
+        ("y_t2", 0, 2),
         ("m1", 3, 2),
-        ("m2", 1, 6),
-        ("y", 1, 6),
-        ("d", 3, 2),
-        ("y_c", 1, 1, "s"),
+        ("m2c", 2, 1, 1),
         ("m1", 3, 3),
-        ("m2", 1, 7),
-        ("y", 1, 7),
-        ("d", 3, 3),
-        ("cast2", 1, 3, "s"),
-        ("store_y", 1, 3),
-        ("store_codes", 0, 0, 4),
-        ("m1", 3, 4),
+        ("y", 1, 2),
         ("m2", 2, 0),
-        ("y", 2, 0),
+        ("d", 3, 1),
+        ("yc", 1, 5),
+        ("store_y", 1, 2),
+        ("cast2", 1, 0, "s"),
+        ("ev", 2, 1, 0, "s"),
+        ("sig", 3, 3),
+        ("y_c", 0, 2, "s"),
+        ("y_t2", 0, 3),
+        ("t1", 1, 6),
+        ("y", 1, 3),
+        ("store_y", 1, 1),
+        ("t1", 1, 7),
+        ("rp2", 3, 0, "v"),
+        ("d", 3, 2),
+        ("yc", 1, 6),
+        ("m1", 3, 4),
+        ("d", 3, 3),
         ("d", 3, 4),
-        ("m1", 3, 5),
+        ("m2c", 2, 1, 2),
         ("m2", 2, 1),
-        ("y", 2, 1),
-        ("d", 3, 5),
-        ("cast2", 2, 0, "s"),
-        ("store_y", 2, 0),
+        ("cast2", 1, 1, "s"),
+        ("y_c", 0, 3, "s"),
+        ("ev", 2, 1, 1, "s"),
+        ("m1", 3, 5),
         ("m1", 3, 6),
         ("m2", 2, 2),
-        ("y", 2, 2),
-        ("d", 3, 6),
+        ("y_t2", 1, 0),
+        ("y_t2", 1, 1),
         ("m1", 3, 7),
-        ("m2", 2, 3),
-        ("y", 2, 3),
-        ("d", 3, 7),
-        ("cast2", 2, 1, "s"),
-        ("store_y", 2, 1),
-        ("m2", 2, 4),
+        ("ev", 2, 1, 2, "s"),
+        ("cast2", 1, 2, "s"),
+        ("y", 2, 0),
         ("y_t2", 1, 2),
+        ("m2c", 2, 1, 3),
+        ("yc", 1, 7),
+        ("store_y", 1, 3),
+        ("cast2", 1, 3, "s"),
+        ("y_c", 1, 0, "s"),
+        ("d", 3, 5),
+        ("y", 2, 1),
+        ("store_y", 2, 0),
+        ("y_q", 0, 0, 4),
+        ("store_codes", 0, 0, 4),
+        ("cast2", 2, 0, "s"),
+        ("y_c", 1, 1, "s"),
+        ("ev", 2, 1, 3, "s"),
+        ("d", 3, 6),
+        ("d", 3, 7),
+        ("m2", 2, 3),
         ("y_t2", 1, 3),
-        ("y", 2, 4),
         ("y_c", 1, 2, "s"),
-        ("y_c", 1, 3, "s"),
+        ("t1", 2, 4),
+        ("y", 2, 2),
         ("d_q", 3),
-        ("m2", 2, 5),
-        ("y_t2", 2, 0),
-        ("y_t2", 2, 1),
-        ("y", 2, 5),
-        ("cast2", 2, 2, "s"),
-        ("store_y", 2, 2),
-        ("y_c", 2, 0, "s"),
-        ("y_q", 1, 0, 4),
-        ("m2", 2, 6),
-        ("y", 2, 6),
-        ("y_c", 2, 1, "s"),
-        ("m2", 2, 7),
-        ("y", 2, 7),
-        ("cast2", 2, 3, "s"),
-        ("store_y", 2, 3),
-        ("store_codes", 1, 0, 4),
+        ("t1", 2, 5),
+        ("m2c", 3, 1, 0),
+        ("m2c", 3, 1, 1),
         ("m2", 3, 0),
-        ("y", 3, 0),
+        ("t1", 2, 6),
+        ("y", 2, 3),
+        ("store_y", 2, 1),
+        ("yc", 2, 4),
+        ("yc", 2, 5),
+        ("store_y", 2, 2),
+        ("y_c", 1, 3, "s"),
+        ("rp2", 3, 1, "v"),
+        ("cast2", 2, 1, "s"),
+        ("ev", 3, 1, 0, "s"),
+        ("ev", 3, 1, 1, "s"),
+        ("cast2", 2, 2, "s"),
+        ("t1", 2, 7),
+        ("m2c", 3, 1, 2),
+        ("y_t2", 2, 0),
+        ("ev", 3, 1, 2, "s"),
+        ("m2c", 3, 1, 3),
+        ("y_c", 2, 0, "s"),
+        ("ev", 3, 1, 3, "s"),
         ("m2", 3, 1),
-        ("y", 3, 1),
-        ("cast2", 3, 0, "s"),
-        ("store_y", 3, 0),
+        ("yc", 2, 6),
+        ("y", 3, 0),
+        ("yc", 2, 7),
+        ("store_y", 2, 3),
         ("m2", 3, 2),
+        ("t1", 3, 4),
+        ("t1", 3, 5),
+        ("cast2", 2, 3, "s"),
+        ("y_q", 1, 0, 4),
+        ("store_codes", 1, 0, 4),
+        ("y_t2", 2, 1),
+        ("m2", 3, 3),
         ("y_t2", 2, 2),
-        ("y_t2", 2, 3),
+        ("t1", 3, 6),
+        ("y", 3, 1),
+        ("store_y", 3, 0),
+        ("cast2", 3, 0, "s"),
         ("y", 3, 2),
+        ("y_t2", 2, 3),
+        ("yc", 3, 4),
+        ("y_c", 2, 1, "s"),
+        ("yc", 3, 5),
+        ("store_y", 3, 2),
         ("y_c", 2, 2, "s"),
         ("y_c", 2, 3, "s"),
-        ("m2", 3, 3),
         ("y", 3, 3),
-        ("cast2", 3, 1, "s"),
         ("store_y", 3, 1),
-        ("m2", 3, 4),
-        ("y", 3, 4),
-        ("m2", 3, 5),
         ("y_t2", 3, 0),
-        ("y", 3, 5),
-        ("cast2", 3, 2, "s"),
-        ("store_y", 3, 2),
+        ("t1", 3, 7),
+        ("yc", 3, 6),
+        ("store_y1", 3, 6),
+        ("cast2", 3, 1, "v"),
         ("y_c", 3, 0, "s"),
+        ("cast1", 3, 6, "s"),
         ("y_q", 2, 0, 4),
         ("store_codes", 2, 0, 4),
         ("store_scales", 0, 3),
-        ("m2", 3, 6),
-        ("y", 3, 6),
-        ("cast1", 3, 6, "s"),
-        ("store_y1", 3, 6),
-        ("m2", 3, 7),
+        ("cast2", 3, 2, "s"),
         ("y_t2", 3, 1),
-        ("y_t2", 3, 2),
-        ("y", 3, 7),
-        ("cast1", 3, 7, "v"),
+        ("y_t1", 3, 6),
+        ("yc", 3, 7),
         ("store_y1", 3, 7),
+        ("y_c1", 3, 6, "v"),
+        ("cast1", 3, 7, "v"),
+        ("y_t2", 3, 2),
         ("y_c", 3, 1, "s"),
-        ("y_c", 3, 2, "v"),
+        ("y_c", 3, 2, "s"),
         ("y_q", 3, 0, 2),
         ("store_codes", 3, 0, 2),
-        ("y_q", 3, 2, 3),
-        ("store_codes", 3, 2, 3),
-        ("y_t1", 3, 6),
-        ("y_c1", 3, 6, "s"),
         ("y_t1", 3, 7),
         ("y_c1", 3, 7, "s"),
+        ("y_q", 3, 2, 3),
+        ("store_codes", 3, 2, 3),
         ("y_q", 3, 3, 4),
         ("store_codes", 3, 3, 4),
         ("store_scales", 3, 4),
@@ -381,6 +397,9 @@ def tile_preconditioned_softplus_gradient_h1_kernel(
         warm = sb.tile([P, 8], F32, name="warm")
         warm2 = sb.tile([P, 8], F32, name="warm2")
         rate_words = sb.tile([P, 16], BF16, name="rate_words")
+        rate_rows = sb.tile([P, P], BF16, name="rate_rows")
+        rate_rows32 = sb.tile([P, P], F32, name="rate_rows32")
+        rate_col = sb.tile([P, 16], F32, name="rate_col")
         rate_all = sb.tile([P, F], BF16, name="rate_all")
         w_scales = {}
         for lo, hi in ((0, 1), (1, 4)):
@@ -440,7 +459,7 @@ def tile_preconditioned_softplus_gradient_h1_kernel(
             nc.sync.dma_start(out=raw(("x", g, dh), [P, 4, 512])[:], in_=rows.rearrange("(p t) d -> p t d", t=4))
 
         def rate_t(h):
-            b = bank(("rate", h), "m2", 3)
+            b = bank(("rate", h), "m2", M2_BANKS)
             words = rate_words[:].bitcast(F32)
             for m in range(4):
                 col = words[:, 4 * h + m : 4 * h + m + 1].to_broadcast([P, P])
@@ -451,7 +470,7 @@ def tile_preconditioned_softplus_gradient_h1_kernel(
             copy(eng, out, live[("rate", h)][:].rearrange("p (m n) -> p n m", m=4))
 
         def rp(c, j, eng):
-            ry = ring(("ry", c, j // 2), "ry", 13, [P, 2, 512], F32)
+            ry = ring(("ry", c, j // 2), "ry", RY, [P, 2, 512], F32)
             engine = nc.gpsimd if eng == "g" else nc.vector
             engine.tensor_tensor(
                 out=ry[:, j % 2, :],
@@ -461,7 +480,7 @@ def tile_preconditioned_softplus_gradient_h1_kernel(
             )
 
         def rp2(c, jj, eng):
-            ry = ring(("ry", c, jj), "ry", 13, [P, 2, 512], F32)
+            ry = ring(("ry", c, jj), "ry", RY, [P, 2, 512], F32)
             engine = nc.gpsimd if eng == "g" else nc.vector
             row = rate_all[:, 512 * c : 512 * (c + 1)].rearrange("p (a f) -> p a f", a=1)
             engine.tensor_tensor(
@@ -485,7 +504,7 @@ def tile_preconditioned_softplus_gradient_h1_kernel(
             )
 
         def y_t2(c, jj):
-            b = bank(("yt", c, jj), "tr", 2)
+            b = bank(("yt", c, jj), "tr", TR_BANKS)
             words = live[("yb2", c, jj)][:].bitcast(F32)
             for i in range(4):
                 nc.tensor.transpose(b[:, P * i : P * (i + 1)], words[:, P * i : P * (i + 1)], ident[:])
@@ -499,7 +518,7 @@ def tile_preconditioned_softplus_gradient_h1_kernel(
             )
 
         def y_t1(c, j):
-            b = bank(("yth", c, j), "tr", 2)
+            b = bank(("yth", c, j), "tr", TR_BANKS)
             words = live[("yb2", c, j // 2)][:].bitcast(F32)
             for u in range(2):
                 i = 2 * (j % 2) + u
@@ -517,8 +536,57 @@ def tile_preconditioned_softplus_gradient_h1_kernel(
             rows = out_0[P * j : P * (j + 1), 512 * c : 512 * (c + 1)]
             nc.sync.dma_start(out=rows, in_=live[("ry", c, j // 2)][:, j % 2, :])
 
+        def load_rrows():
+            nc.vector.memset(rate_rows[:], 0.0)
+            nc.sync.dma_start(out=rate_rows[0:16, :], in_=rate.rearrange("(q p) -> q p", p=P))
+
+        def rcol_cast():
+            nc.vector.tensor_copy(out=rate_rows32[:], in_=rate_rows[:])
+
+        def rcol_t():
+            b = bank("rcol", "m2", M2_BANKS)
+            nc.tensor.transpose(b[:, 0:P], rate_rows32[:], ident[:])
+
+        def rcol_c(eng):
+            copy(eng, rate_col[:], live["rcol"][:, 0:16])
+
+        def m2c(c, dh, s):
+            b = bank(("m2c", c, dh, s), "m2", M2_BANKS)
+            for g in range(2):
+                cols = slice(512 * g + P * s, 512 * g + P * (s + 1))
+                nc.tensor.matmul_mx(
+                    out=b[:],
+                    lhsT=live[("dc", c)][:, cols].bitcast(FP8X4),
+                    lhsT_scale=live[("ds", c)][:, cols],
+                    rhs=x_codes[:, dh, 512 * g : 512 * (g + 1)].bitcast(FP8X4),
+                    rhs_scale=x_scales[:, dh, 512 * g : 512 * (g + 1)],
+                    start=(g == 0),
+                    stop=(g == 1),
+                )
+
+        def ev(c, dh, s, eng):
+            out = ring(("gr", c, dh, s), "gr", 7, [P, 512], F32)
+            factor = rate_col[:, 4 * c + s : 4 * c + s + 1]
+            b = live[("m2c", c, dh, s)]
+            if eng == "s":
+                nc.scalar.activation(out=out[:], in_=b[:], func=COPY, scale=factor)
+            else:
+                nc.vector.tensor_scalar(out=out[:], in0=b[:], scalar1=factor, scalar2=None, op0=MULT)
+
+        def t1(c, j):
+            b = bank(("t1", c, j), "tr", TR_BANKS)
+            dh, a = divmod(j, 4)
+            for s in range(4):
+                nc.tensor.transpose(b[:, P * s : P * (s + 1)], live[("gr", c, dh, s)][:, P * a : P * (a + 1)], ident[:])
+
+        def yc(c, j):
+            ry = ring(("ry", c, j // 2), "ry", RY, [P, 2, 512], F32)
+            nc.vector.tensor_tensor(
+                out=ry[:, j % 2, :], in0=live[("t1", c, j)][:], in1=live[("p", c, j // 4)][:, j % 4, :], op=MULT
+            )
+
         def e_t(g, t):
-            b = bank(("et", g, t), "tr", 2) if t % 2 == 0 else bank(("et", g, t), "m2", 3)
+            b = bank(("et", g, t), "tr", TR_BANKS) if t % 2 == 0 else bank(("et", g, t), "m2", M2_BANKS)
             words = live[("e", g, t // 2)][:].bitcast(F32)
             for c in range(2):
                 for u in range(2):
@@ -555,7 +623,7 @@ def tile_preconditioned_softplus_gradient_h1_kernel(
 
         def m1(c, k):
             g, s = divmod(k, 4)
-            b = bank(("m1", c, k), "m1", 3)
+            b = bank(("m1", c, k), "m1", M1_BANKS)
             words, w0 = w_words[c]
             plane, s0 = w_scales[c]
             w0 = 2 * (512 * (c - w0) + P * s)
@@ -605,7 +673,7 @@ def tile_preconditioned_softplus_gradient_h1_kernel(
             )
 
         def m2(c, j):
-            b = bank(("m2", c, j), "m2", 3)
+            b = bank(("m2", c, j), "m2", M2_BANKS)
             dh, a = divmod(j, 4)
             for g in range(2):
                 cols = slice(512 * g + P * a, 512 * g + P * (a + 1))
@@ -632,7 +700,7 @@ def tile_preconditioned_softplus_gradient_h1_kernel(
             )
 
         def y_t(c, jj):
-            b = bank(("yt", c, jj), "tr", 2)
+            b = bank(("yt", c, jj), "tr", TR_BANKS)
             for a in range(2):
                 words = live[("yb", c, 2 * jj + a)][:].bitcast(F32)
                 for u in range(2):
@@ -674,7 +742,7 @@ def tile_preconditioned_softplus_gradient_h1_kernel(
 
         steps = {
             "load_rate": load_rate, "load_e": load_e, "load_wsc": load_wsc, "load_w": load_w, "load_z": load_z,
-            "load_p": load_p, "load_x": load_x, "rate_t": rate_t, "rate_c": rate_c, "rp": rp, "cast1": cast1, "y_t1": y_t1, "y_c1": y_c1, "store_y1": store_y1, "rp2": rp2, "e_q4": e_q4, "cast2": cast2, "y_t2": y_t2, "e_t": e_t,
+            "load_p": load_p, "load_x": load_x, "rate_t": rate_t, "rate_c": rate_c, "rp": rp, "load_rrows": load_rrows, "rcol_cast": rcol_cast, "rcol_t": rcol_t, "rcol_c": rcol_c, "m2c": m2c, "ev": ev, "t1": t1, "yc": yc, "cast1": cast1, "y_t1": y_t1, "y_c1": y_c1, "store_y1": store_y1, "rp2": rp2, "e_q4": e_q4, "cast2": cast2, "y_t2": y_t2, "e_t": e_t,
             "e_c": e_c, "e_q": e_q, "sig": sig, "m1": m1, "d": d, "d_q": d_q, "x_i": x_i, "x_q": x_q, "m2": m2,
             "y": y, "cast": cast, "y_t": y_t, "y_c": y_c, "y_q": y_q, "store_y": store_y,
             "store_codes": store_codes, "store_scales": store_scales,

from contextlib import ExitStack

import concourse.mybir as mybir
from concourse.masks import make_identity

T, C, F, D = 1024, 1024, 2048, 1024
FLOPS = 2 * T * C * F + 2 * T * D * F

F32 = mybir.dt.float32
BF16 = mybir.dt.bfloat16
I32 = mybir.dt.int32
U32 = mybir.dt.uint32
U8 = mybir.dt.uint8
FP8X4 = mybir.dt.float8_e4m3fn_x4
FP4X4 = mybir.dt.float4_e2m1fn_x4
MULT = mybir.AluOpType.mult
ADD = mybir.AluOpType.add
SIGMOID = mybir.ActivationFunctionType.Sigmoid

COPY = mybir.ActivationFunctionType.Copy

P = 128
M1_BANKS, M2_BANKS, TR_BANKS = 2, 3, 3
RY = 10
CHUNKS = 4


def plan():
    return [
        ("load_e", 0, 0),
        ("load_e", 0, 1),
        ("load_rate",),
        ("load_x", 0, 0),
        ("load_e", 1, 0),
        ("load_wsc", 0, 1),
        ("load_x", 1, 0),
        ("load_w", 0, 1),
        ("load_z", 0, 0),
        ("load_e", 1, 1),
        ("load_rrows",),
        ("load_z", 0, 1),
        ("load_w", 1, 2),
        ("load_wsc", 1, 4),
        ("load_z", 1, 0),
        ("load_p", 0, 0),
        ("load_x", 0, 1),
        ("load_w", 2, 4),
        ("load_x", 1, 1),
        ("load_p", 0, 1),
        ("load_p", 1, 0),
        ("load_z", 1, 1),
        ("load_z", 2, 0),
        ("load_p", 1, 1),
        ("load_z", 2, 1),
        ("load_z", 3, 0),
        ("load_p", 2, 0),
        ("load_z", 3, 1),
        ("load_p", 2, 1),
        ("load_p", 3, 0),
        ("load_p", 3, 1),
        ("e_t", 0, 0),
        ("e_c", 0, 0, "v"),
        ("e_t", 0, 1),
        ("e_c", 0, 1, "s"),
        ("x_i", 0, 0, 0, "v"),
        ("e_t", 0, 2),
        ("e_t", 0, 3),
        ("e_t", 1, 0),
        ("e_c", 0, 2, "s"),
        ("e_c", 0, 3, "s"),
        ("rate_t", 0),
        ("e_t", 1, 1),
        ("x_i", 0, 0, 1, "v"),
        ("e_q4", 0),
        ("m1", 0, 0),
        ("rate_c", 0, "s"),
        ("e_c", 1, 0, "s"),
        ("e_t", 1, 2),
        ("e_c", 1, 1, "s"),
        ("e_t", 1, 3),
        ("m1", 0, 1),
        ("sig", 0, 0),
        ("x_i", 1, 0, 0, "v"),
        ("x_i", 1, 0, 1, "v"),
        ("rate_t", 1),
        ("m1", 0, 2),
        ("sig", 0, 1),
        ("e_c", 1, 2, "s"),
        ("sig", 0, 2),
        ("m1", 0, 3),
        ("x_q", 0),
        ("sig", 0, 3),
        ("rcol_cast",),
        ("d", 0, 0),
        ("e_c", 1, 3, "v"),
        ("d", 0, 1),
        ("e_q4", 1),
        ("d", 0, 2),
        ("m1", 0, 4),
        ("m1", 0, 5),
        ("rate_c", 1, "s"),
        ("d", 0, 3),
        ("sig", 1, 0),
        ("rcol_t",),
        ("m1", 0, 6),
        ("x_i", 0, 1, 0, "s"),
        ("m1", 0, 7),
        ("d", 0, 4),
        ("x_i", 0, 1, 1, "s"),
        ("d", 0, 5),
        ("rp2", 0, 0, "v"),
        ("d", 0, 6),
        ("x_i", 1, 1, 0, "s"),
        ("d", 0, 7),
        ("rp2", 0, 1, "v"),
        ("m1", 1, 0),
        ("d", 1, 0),
        ("m1", 1, 1),
        ("m1", 1, 2),
        ("d", 1, 1),
        ("d_q", 0),
        ("m1", 1, 3),
        ("x_i", 1, 1, 1, "s"),
        ("x_q", 1),
        ("sig", 1, 1),
        ("m2", 0, 0),
        ("m2c", 0, 1, 0),
        ("m1", 1, 4),
        ("m2", 0, 1),
        ("m1", 1, 5),
        ("m2c", 0, 1, 1),
        ("d", 1, 2),
        ("y", 0, 0),
        ("m2", 0, 2),
        ("m1", 1, 6),
        ("d", 1, 3),
        ("sig", 1, 2),
        ("sig", 1, 3),
        ("m1", 1, 7),
        ("d", 1, 4),
        ("rp2", 1, 0, "v"),
        ("m2", 0, 3),
        ("m2c", 0, 1, 2),
        ("d", 1, 5),
        ("m1", 2, 0),
        ("m1", 2, 1),
        ("m2c", 0, 1, 3),
        ("rcol_c", "s"),
        ("m1", 2, 2),
        ("ev", 0, 1, 0, "s"),
        ("sig", 2, 0),
        ("y", 0, 1),
        ("store_y", 0, 0),
        ("sig", 2, 1),
        ("ev", 0, 1, 1, "s"),
        ("d", 1, 6),
        ("cast2", 0, 0, "s"),
        ("sig", 2, 2),
        ("ev", 0, 1, 2, "s"),
        ("d", 1, 7),
        ("y", 0, 2),
        ("d_q", 1),
        ("d", 2, 0),
        ("m1", 2, 3),
        ("m2c", 1, 1, 0),
        ("m2", 1, 0),
        ("sig", 2, 3),
        ("ev", 0, 1, 3, "s"),
        ("m2c", 1, 1, 1),
        ("d", 2, 1),
        ("m1", 2, 4),
        ("y", 0, 3),
        ("store_y", 0, 1),
        ("t1", 0, 4),
        ("y_t2", 0, 0),
        ("d", 2, 2),
        ("rp2", 1, 1, "v"),
        ("t1", 0, 5),
        ("m1", 2, 5),
        ("m2c", 1, 1, 2),
        ("m1", 2, 6),
        ("rp2", 2, 0, "v"),
        ("d", 2, 3),
        ("cast2", 0, 1, "s"),
        ("ev", 1, 1, 0, "s"),
        ("ev", 1, 1, 1, "s"),
        ("sig", 3, 0),
        ("y_c", 0, 0, "s"),
        ("sig", 3, 1),
        ("yc", 0, 4),
        ("d", 2, 4),
        ("y", 1, 0),
        ("d", 2, 5),
        ("yc", 0, 5),
        ("store_y", 0, 2),
        ("rp2", 2, 1, "v"),
        ("m2c", 1, 1, 3),
        ("t1", 0, 6),
        ("y_t2", 0, 1),
        ("t1", 0, 7),
        ("m1", 2, 7),
        ("m2", 1, 1),
        ("yc", 0, 6),
        ("d", 2, 6),
        ("d", 2, 7),
        ("ev", 1, 1, 2, "s"),
        ("cast2", 0, 2, "s"),
        ("ev", 1, 1, 3, "s"),
        ("sig", 3, 2),
        ("y_c", 0, 1, "s"),
        ("yc", 0, 7),
        ("store_y", 0, 3),
        ("m2", 1, 2),
        ("m2", 1, 3),
        ("m1", 3, 0),
        ("t1", 1, 4),
        ("d_q", 2),
        ("d", 3, 0),
        ("t1", 1, 5),
        ("y", 1, 1),
        ("store_y", 1, 0),
        ("m1", 3, 1),
        ("cast2", 0, 3, "s"),
        ("yc", 1, 4),
        ("m2c", 2, 1, 0),
        ("y_t2", 0, 2),
        ("m1", 3, 2),
        ("m2c", 2, 1, 1),
        ("m1", 3, 3),
        ("y", 1, 2),
        ("m2", 2, 0),
        ("d", 3, 1),
        ("yc", 1, 5),
        ("store_y", 1, 2),
        ("cast2", 1, 0, "s"),
        ("ev", 2, 1, 0, "s"),
        ("sig", 3, 3),
        ("y_c", 0, 2, "s"),
        ("y_t2", 0, 3),
        ("t1", 1, 6),
        ("y", 1, 3),
        ("store_y", 1, 1),
        ("t1", 1, 7),
        ("rp2", 3, 0, "v"),
        ("d", 3, 2),
        ("yc", 1, 6),
        ("m1", 3, 4),
        ("d", 3, 3),
        ("d", 3, 4),
        ("m2c", 2, 1, 2),
        ("m2", 2, 1),
        ("cast2", 1, 1, "s"),
        ("y_c", 0, 3, "s"),
        ("ev", 2, 1, 1, "s"),
        ("m1", 3, 5),
        ("m1", 3, 6),
        ("m2", 2, 2),
        ("y_t2", 1, 0),
        ("y_t2", 1, 1),
        ("m1", 3, 7),
        ("ev", 2, 1, 2, "s"),
        ("cast2", 1, 2, "s"),
        ("y", 2, 0),
        ("y_t2", 1, 2),
        ("m2c", 2, 1, 3),
        ("yc", 1, 7),
        ("store_y", 1, 3),
        ("cast2", 1, 3, "s"),
        ("y_c", 1, 0, "s"),
        ("d", 3, 5),
        ("y", 2, 1),
        ("store_y", 2, 0),
        ("y_q", 0, 0, 4),
        ("store_codes", 0, 0, 4),
        ("cast2", 2, 0, "s"),
        ("y_c", 1, 1, "s"),
        ("ev", 2, 1, 3, "s"),
        ("d", 3, 6),
        ("d", 3, 7),
        ("m2", 2, 3),
        ("y_t2", 1, 3),
        ("y_c", 1, 2, "s"),
        ("t1", 2, 4),
        ("y", 2, 2),
        ("d_q", 3),
        ("t1", 2, 5),
        ("m2c", 3, 1, 0),
        ("m2c", 3, 1, 1),
        ("m2", 3, 0),
        ("t1", 2, 6),
        ("y", 2, 3),
        ("store_y", 2, 1),
        ("yc", 2, 4),
        ("yc", 2, 5),
        ("store_y", 2, 2),
        ("y_c", 1, 3, "s"),
        ("rp2", 3, 1, "v"),
        ("cast2", 2, 1, "s"),
        ("ev", 3, 1, 0, "s"),
        ("ev", 3, 1, 1, "s"),
        ("cast2", 2, 2, "s"),
        ("t1", 2, 7),
        ("m2c", 3, 1, 2),
        ("y_t2", 2, 0),
        ("ev", 3, 1, 2, "s"),
        ("m2c", 3, 1, 3),
        ("y_c", 2, 0, "s"),
        ("ev", 3, 1, 3, "s"),
        ("m2", 3, 1),
        ("yc", 2, 6),
        ("y", 3, 0),
        ("yc", 2, 7),
        ("store_y", 2, 3),
        ("m2", 3, 2),
        ("t1", 3, 4),
        ("t1", 3, 5),
        ("cast2", 2, 3, "s"),
        ("y_q", 1, 0, 4),
        ("store_codes", 1, 0, 4),
        ("y_t2", 2, 1),
        ("m2", 3, 3),
        ("y_t2", 2, 2),
        ("t1", 3, 6),
        ("y", 3, 1),
        ("store_y", 3, 0),
        ("cast2", 3, 0, "s"),
        ("y", 3, 2),
        ("y_t2", 2, 3),
        ("yc", 3, 4),
        ("y_c", 2, 1, "s"),
        ("yc", 3, 5),
        ("store_y", 3, 2),
        ("y_c", 2, 2, "s"),
        ("y_c", 2, 3, "s"),
        ("y", 3, 3),
        ("store_y", 3, 1),
        ("y_t2", 3, 0),
        ("t1", 3, 7),
        ("yc", 3, 6),
        ("store_y1", 3, 6),
        ("cast2", 3, 1, "v"),
        ("y_c", 3, 0, "s"),
        ("cast1", 3, 6, "s"),
        ("y_q", 2, 0, 4),
        ("store_codes", 2, 0, 4),
        ("store_scales", 0, 3),
        ("cast2", 3, 2, "s"),
        ("y_t2", 3, 1),
        ("y_t1", 3, 6),
        ("yc", 3, 7),
        ("store_y1", 3, 7),
        ("y_c1", 3, 6, "v"),
        ("cast1", 3, 7, "v"),
        ("y_t2", 3, 2),
        ("y_c", 3, 1, "s"),
        ("y_c", 3, 2, "s"),
        ("y_q", 3, 0, 2),
        ("store_codes", 3, 0, 2),
        ("y_t1", 3, 7),
        ("y_c1", 3, 7, "s"),
        ("y_q", 3, 2, 3),
        ("store_codes", 3, 2, 3),
        ("y_q", 3, 3, 4),
        ("store_codes", 3, 3, 4),
        ("store_scales", 3, 4),
    ]


def tile_preconditioned_softplus_gradient_h1_kernel(
    tc, errors, wt_words, wt_scales, preact, x, rate, precond, out_0, out_1, out_2
):
    nc = tc.nc
    with ExitStack() as ctx:
        sb = ctx.enter_context(tc.tile_pool(name="sb", bufs=1))
        psum = ctx.enter_context(tc.psum_pool(name="psum", bufs=1))
        ctx.enter_context(tc.manual_schedule())
        live = {}

        def ring(key, tag, bufs, shape, dtype):
            if key not in live:
                live[key] = sb.tile(shape, dtype, name=tag, tag=tag, bufs=bufs, align_bytes=64)
            return live[key]

        def bank(key, tag, bufs):
            live[key] = psum.tile([P, 512], F32, name=tag, tag=tag, bufs=bufs)
            return live[key]

        def copy(eng, out, in_):
            if eng == "v":
                nc.vector.tensor_copy(out=out, in_=in_)
            elif eng == "s":
                nc.scalar.copy(out=out, in_=in_)
            else:
                nc.gpsimd.tensor_scalar(out=out, in0=in_, scalar1=1.0, scalar2=-0.0, op0=MULT, op1=ADD)

        ident = sb.tile([P, P], F32, name="ident")
        warm = sb.tile([P, 8], F32, name="warm")
        warm2 = sb.tile([P, 8], F32, name="warm2")
        rate_words = sb.tile([P, 16], BF16, name="rate_words")
        rate_rows = sb.tile([P, P], BF16, name="rate_rows")
        rate_rows32 = sb.tile([P, P], F32, name="rate_rows32")
        rate_col = sb.tile([P, 16], F32, name="rate_col")
        rate_all = sb.tile([P, F], BF16, name="rate_all")
        w_scales = {}
        for lo, hi in ((0, 1), (1, 4)):
            plane = sb.tile([P, 2, 512 * (hi - lo)], U8, name="w_scales_%d" % lo, align_bytes=64)
            for c in range(lo, hi):
                w_scales[c] = (plane, lo)
        w_words = {}
        for lo, hi in ((0, 1), (1, 2), (2, 4)):
            words = sb.tile([P, 2, 1024 * (hi - lo)], U8, name="w_words_%d" % lo, align_bytes=64)
            for c in range(lo, hi):
                w_words[c] = (words, lo)
        e_codes = sb.tile([P, 2, 1024], U32, name="e_codes", align_bytes=64)
        e_scales = sb.tile([P, 2, 1024], U8, name="e_scales", align_bytes=64)
        x_codes = sb.tile([P, 2, 1024], U32, name="x_codes", align_bytes=64)
        x_scales = sb.tile([P, 2, 1024], U8, name="x_scales", align_bytes=64)
        y_scales = sb.tile([P, CHUNKS, D], U8, name="y_scales", align_bytes=64)

        for c in (0, 1):
            nc.vector.memset(w_scales[c][0][:].rearrange("p g n -> p (g n)").bitcast(I32), 0)
        nc.vector.memset(warm[:], 0.0)
        nc.scalar.activation(out=warm2[:], in_=warm[:], func=SIGMOID)
        make_identity(nc, ident[:])

        def raw(key, shape):
            return ring(key, "raw", 16, shape, BF16)

        def load_rate():
            nc.sync.dma_start(out=rate_words[:], in_=rate.rearrange("(p m) -> p m", p=P))

        def load_e(g, h):
            rows = errors[512 * g : 512 * (g + 1), :].rearrange("(m t) k -> m t k", t=4)
            nc.sync.dma_start(out=raw(("e", g, h), [P, 2, C])[:], in_=rows[:, 2 * h : 2 * h + 2, :])

        def load_wsc(lo, hi):
            cols = slice(512 * lo, 512 * hi)
            for q in range(4):
                nc.sync.dma_start(
                    out=w_scales[lo][0][32 * q : 32 * q + 4, :, :].bitcast(I32),
                    in_=wt_scales[:, 4 * q : 4 * q + 4, cols].rearrange("g r n -> r g n").bitcast(I32),
                )

        def load_w(lo, hi):
            cols = slice(1024 * lo, 1024 * hi)
            words = wt_words.rearrange("g p n -> p g n")
            nc.sync.dma_start(out=w_words[lo][0][:].bitcast(I32), in_=words[:, :, cols].bitcast(I32))

        def load_z(c, g):
            rows = preact[512 * g : 512 * (g + 1), 512 * c : 512 * (c + 1)]
            nc.sync.dma_start(out=raw(("z", c, g), [P, 4, 512])[:], in_=rows.rearrange("(p t) f -> p t f", t=4))

        def load_p(c, h):
            rows = precond[512 * h : 512 * (h + 1), 512 * c : 512 * (c + 1)]
            nc.sync.dma_start(out=raw(("p", c, h), [P, 4, 512])[:], in_=rows.rearrange("(a p) f -> p a f", p=P))

        def load_x(g, dh):
            rows = x[512 * g : 512 * (g + 1), 512 * dh : 512 * (dh + 1)]
            nc.sync.dma_start(out=raw(("x", g, dh), [P, 4, 512])[:], in_=rows.rearrange("(p t) d -> p t d", t=4))

        def rate_t(h):
            b = bank(("rate", h), "m2", M2_BANKS)
            words = rate_words[:].bitcast(F32)
            for m in range(4):
                col = words[:, 4 * h + m : 4 * h + m + 1].to_broadcast([P, P])
                nc.tensor.transpose(b[:, P * m : P * (m + 1)], col, ident[:])

        def rate_c(h, eng):
            out = rate_all[:].bitcast(F32).rearrange("p (n m) -> p n m", m=8)[:, :, 4 * h : 4 * h + 4]
            copy(eng, out, live[("rate", h)][:].rearrange("p (m n) -> p n m", m=4))

        def rp(c, j, eng):
            ry = ring(("ry", c, j // 2), "ry", RY, [P, 2, 512], F32)
            engine = nc.gpsimd if eng == "g" else nc.vector
            engine.tensor_tensor(
                out=ry[:, j % 2, :],
                in0=live[("p", c, j // 4)][:, j % 4, :],
                in1=rate_all[:, 512 * c : 512 * (c + 1)],
                op=MULT,
            )

        def rp2(c, jj, eng):
            ry = ring(("ry", c, jj), "ry", RY, [P, 2, 512], F32)
            engine = nc.gpsimd if eng == "g" else nc.vector
            row = rate_all[:, 512 * c : 512 * (c + 1)].rearrange("p (a f) -> p a f", a=1)
            engine.tensor_tensor(
                out=ry[:],
                in0=live[("p", c, jj // 2)][:, 2 * (jj % 2) : 2 * (jj % 2) + 2, :],
                in1=row.to_broadcast([P, 2, 512]),
                op=MULT,
            )

        def e_q4(g):
            nc.vector.quantize_mx(
                out=e_codes[:, g, :].bitcast(FP8X4), scales=e_scales[:, g, :], in_=live[("eT", g)][:]
            )

        def cast2(c, jj, eng):
            yb = ring(("yb2", c, jj), "yb2", 4, [P, 1024], BF16)
            copy(
                eng,
                yb[:].rearrange("p (a u m e) -> p a u m e", a=2, u=2, e=2),
                live[("ry", c, jj)][:].rearrange("p a (m u e) -> p a u m e", u=2, e=2),
            )

        def y_t2(c, jj):
            b = bank(("yt", c, jj), "tr", TR_BANKS)
            words = live[("yb2", c, jj)][:].bitcast(F32)
            for i in range(4):
                nc.tensor.transpose(b[:, P * i : P * (i + 1)], words[:, P * i : P * (i + 1)], ident[:])

        def cast1(c, j, eng):
            yb = ring(("yb2", c, j // 2), "yb2", 4, [P, 1024], BF16)[:, 512 * (j % 2) : 512 * (j % 2 + 1)]
            copy(
                eng,
                yb.rearrange("p (u m e) -> p u m e", u=2, e=2),
                live[("ry", c, j // 2)][:, j % 2, :].rearrange("p (m u e) -> p u m e", u=2, e=2),
            )

        def y_t1(c, j):
            b = bank(("yth", c, j), "tr", TR_BANKS)
            words = live[("yb2", c, j // 2)][:].bitcast(F32)
            for u in range(2):
                i = 2 * (j % 2) + u
                nc.tensor.transpose(b[:, P * u : P * (u + 1)], words[:, P * i : P * (i + 1)], ident[:])

        def y_c1(c, j, eng):
            dst = ring(("yT", c), "qb", 2, [P, 4096], BF16)[:].bitcast(F32)[:, 256 * j : 256 * (j + 1)]
            copy(
                eng,
                dst.rearrange("p (d u) -> p d u", u=2),
                live[("yth", c, j)][:, 0:256].rearrange("p (u d) -> p d u", u=2),
            )

        def store_y1(c, j):
            rows = out_0[P * j : P * (j + 1), 512 * c : 512 * (c + 1)]
            nc.sync.dma_start(out=rows, in_=live[("ry", c, j // 2)][:, j % 2, :])

        def load_rrows():
            nc.vector.memset(rate_rows[:], 0.0)
            nc.sync.dma_start(out=rate_rows[0:16, :], in_=rate.rearrange("(q p) -> q p", p=P))

        def rcol_cast():
            nc.vector.tensor_copy(out=rate_rows32[:], in_=rate_rows[:])

        def rcol_t():
            b = bank("rcol", "m2", M2_BANKS)
            nc.tensor.transpose(b[:, 0:P], rate_rows32[:], ident[:])

        def rcol_c(eng):
            copy(eng, rate_col[:], live["rcol"][:, 0:16])

        def m2c(c, dh, s):
            b = bank(("m2c", c, dh, s), "m2", M2_BANKS)
            for g in range(2):
                cols = slice(512 * g + P * s, 512 * g + P * (s + 1))
                nc.tensor.matmul_mx(
                    out=b[:],
                    lhsT=live[("dc", c)][:, cols].bitcast(FP8X4),
                    lhsT_scale=live[("ds", c)][:, cols],
                    rhs=x_codes[:, dh, 512 * g : 512 * (g + 1)].bitcast(FP8X4),
                    rhs_scale=x_scales[:, dh, 512 * g : 512 * (g + 1)],
                    start=(g == 0),
                    stop=(g == 1),
                )

        def ev(c, dh, s, eng):
            out = ring(("gr", c, dh, s), "gr", 7, [P, 512], F32)
            factor = rate_col[:, 4 * c + s : 4 * c + s + 1]
            b = live[("m2c", c, dh, s)]
            if eng == "s":
                nc.scalar.activation(out=out[:], in_=b[:], func=COPY, scale=factor)
            else:
                nc.vector.tensor_scalar(out=out[:], in0=b[:], scalar1=factor, scalar2=None, op0=MULT)

        def t1(c, j):
            b = bank(("t1", c, j), "tr", TR_BANKS)
            dh, a = divmod(j, 4)
            for s in range(4):
                nc.tensor.transpose(b[:, P * s : P * (s + 1)], live[("gr", c, dh, s)][:, P * a : P * (a + 1)], ident[:])

        def yc(c, j):
            ry = ring(("ry", c, j // 2), "ry", RY, [P, 2, 512], F32)
            nc.vector.tensor_tensor(
                out=ry[:, j % 2, :], in0=live[("t1", c, j)][:], in1=live[("p", c, j // 4)][:, j % 4, :], op=MULT
            )

        def e_t(g, t):
            b = bank(("et", g, t), "tr", TR_BANKS) if t % 2 == 0 else bank(("et", g, t), "m2", M2_BANKS)
            words = live[("e", g, t // 2)][:].bitcast(F32)
            for c in range(2):
                for u in range(2):
                    i = 2 * c + u
                    nc.tensor.transpose(
                        b[:, P * i : P * (i + 1)], words[:, t % 2, 256 * c + u : 256 * (c + 1) : 2], ident[:]
                    )

        def e_c(g, t, eng):
            dst = ring(("eT", g), "qa" if g == 0 else "qb", 2, [P, 4096], BF16)[:].bitcast(F32)[:, 512 * t : 512 * (t + 1)]
            copy(
                eng,
                dst.rearrange("p (c m u) -> p c m u", c=2, u=2),
                live[("et", g, t)][:].rearrange("p (c u m) -> p c m u", c=2, u=2),
            )

        def e_q(g, h):
            cols = slice(512 * h, 512 * (h + 1))
            nc.vector.quantize_mx(
                out=e_codes[:, g, cols].bitcast(FP8X4),
                scales=e_scales[:, g, cols],
                in_=live[("eT", g)][:, 2048 * h : 2048 * (h + 1)],
            )

        def sig(c, i):
            g, h = divmod(i, 2)
            out = ring(("sig", c, i), "sig", 4, [P, 1024], F32)
            z = live[("z", c, g)][:, :, 256 * h : 256 * (h + 1)]
            nc.scalar.activation(
                out=out[:].rearrange("p (u f e) -> p u f e", u=2, e=2),
                in_=z.rearrange("p (u e) f -> p u f e", u=2),
                func=SIGMOID,
            )

        def m1(c, k):
            g, s = divmod(k, 4)
            b = bank(("m1", c, k), "m1", M1_BANKS)
            words, w0 = w_words[c]
            plane, s0 = w_scales[c]
            w0 = 2 * (512 * (c - w0) + P * s)
            s0 = 512 * (c - s0) + P * s
            for t in range(4):
                for h in range(2):
                    cols = slice(256 * t + P * h, 256 * t + P * (h + 1))
                    w = words[:, h, w0 : w0 + 256]
                    nc.tensor.matmul_mx(
                        out=b[:, P * t : P * (t + 1)],
                        lhsT=e_codes[:, g, cols].bitcast(FP8X4),
                        lhsT_scale=e_scales[:, g, cols],
                        rhs=w.bitcast(FP4X4),
                        rhs_scale=plane[:, h, s0 : s0 + P],
                        start=(h == 0),
                        stop=(h == 1),
                    )

        def d(c, k):
            g, s = divmod(k, 4)
            dl = ring(("dl", c), "qa", 2, [P, 4096], BF16)
            gate = live[("sig", c, k // 2)][:].rearrange("p (u f e) -> p f u e", u=2, e=2)
            nc.vector.tensor_tensor(
                out=dl[:, 512 * k : 512 * (k + 1)].rearrange("p (f u e) -> p f u e", u=2, e=2),
                in0=gate[:, P * (k % 2) : P * (k % 2 + 1), :, :],
                in1=live[("m1", c, k)][:].rearrange("p (u e f) -> p f u e", u=2, e=2),
                op=MULT,
            )

        def d_q(c):
            codes = ring(("dc", c), "d_codes", 2, [P, 1024], U32)
            scales = ring(("ds", c), "d_scales", 2, [P, 1024], U8)
            nc.vector.quantize_mx(out=codes[:].bitcast(FP8X4), scales=scales[:], in_=live[("dl", c)][:])

        def x_i(g, dh, q, eng):
            dst = ring(("xi", dh), "qb", 2, [P, 4096], BF16)[:, 2048 * g + 1024 * q : 2048 * g + 1024 * (q + 1)]
            src = live[("x", g, dh)][:, :, 256 * q : 256 * (q + 1)]
            copy(
                eng,
                dst.rearrange("p (c i t) -> p c t i", i=4, t=4),
                src.rearrange("p t (c i) -> p c t i", i=4),
            )

        def x_q(dh):
            nc.vector.quantize_mx(
                out=x_codes[:, dh, :].bitcast(FP8X4), scales=x_scales[:, dh, :], in_=live[("xi", dh)][:]
            )

        def m2(c, j):
            b = bank(("m2", c, j), "m2", M2_BANKS)
            dh, a = divmod(j, 4)
            for g in range(2):
                cols = slice(512 * g + P * a, 512 * g + P * (a + 1))
                nc.tensor.matmul_mx(
                    out=b[:],
                    lhsT=x_codes[:, dh, cols].bitcast(FP8X4),
                    lhsT_scale=x_scales[:, dh, cols],
                    rhs=live[("dc", c)][:, 512 * g : 512 * (g + 1)].bitcast(FP8X4),
                    rhs_scale=live[("ds", c)][:, 512 * g : 512 * (g + 1)],
                    start=(g == 0),
                    stop=(g == 1),
                )

        def y(c, j):
            ry = live[("ry", c, j // 2)][:, j % 2, :]
            nc.vector.tensor_tensor(out=ry, in0=ry, in1=live[("m2", c, j)][:], op=MULT)

        def cast(c, j, eng):
            yb = ring(("yb", c, j), "yb", 8, [P, 512], BF16)
            copy(
                eng,
                yb[:].rearrange("p (u m e) -> p u m e", u=2, e=2),
                live[("ry", c, j // 2)][:, j % 2, :].rearrange("p (m u e) -> p u m e", u=2, e=2),
            )

        def y_t(c, jj):
            b = bank(("yt", c, jj), "tr", TR_BANKS)
            for a in range(2):
                words = live[("yb", c, 2 * jj + a)][:].bitcast(F32)
                for u in range(2):
                    i = 2 * a + u
                    nc.tensor.transpose(b[:, P * i : P * (i + 1)], words[:, P * u : P * (u + 1)], ident[:])

        def y_c(c, jj, eng):
            dst = ring(("yT", c), "qb", 2, [P, 4096], BF16)[:].bitcast(F32)[:, 512 * jj : 512 * (jj + 1)]
            copy(
                eng,
                dst.rearrange("p (a d u) -> p a d u", a=2, u=2),
                live[("yt", c, jj)][:].rearrange("p (a u d) -> p a d u", a=2, u=2),
            )

        def y_q(c, lo, hi):
            codes = ring(("yc", c), "y_codes", 2, [P, D], U32)
            cols = slice(256 * lo, 256 * hi)
            nc.vector.quantize_mx(
                out=codes[:, cols].bitcast(FP8X4),
                scales=y_scales[:, c, cols],
                in_=live[("yT", c)][:, 1024 * lo : 1024 * hi],
            )

        def store_y(c, jj):
            rows = out_0[256 * jj : 256 * (jj + 1), 512 * c : 512 * (c + 1)]
            nc.sync.dma_start(out=rows.rearrange("(a p) f -> p a f", p=P), in_=live[("ry", c, jj)][:])

        def store_codes(c, lo, hi):
            cols = slice(256 * lo, 256 * hi)
            words = out_1[c].rearrange("p m t -> p (m t)").bitcast(I32)
            nc.sync.dma_start(out=words[:, cols], in_=live[("yc", c)][:, cols].bitcast(I32))

        def store_scales(lo, hi):
            for q in range(4):
                nc.sync.dma_start(
                    out=out_2[lo:hi, 4 * q : 4 * q + 4, :].rearrange("g r m -> r g m").bitcast(I32),
                    in_=y_scales[32 * q : 32 * q + 4, lo:hi, :].bitcast(I32),
                )

        steps = {
            "load_rate": load_rate, "load_e": load_e, "load_wsc": load_wsc, "load_w": load_w, "load_z": load_z,
            "load_p": load_p, "load_x": load_x, "rate_t": rate_t, "rate_c": rate_c, "rp": rp, "load_rrows": load_rrows, "rcol_cast": rcol_cast, "rcol_t": rcol_t, "rcol_c": rcol_c, "m2c": m2c, "ev": ev, "t1": t1, "yc": yc, "cast1": cast1, "y_t1": y_t1, "y_c1": y_c1, "store_y1": store_y1, "rp2": rp2, "e_q4": e_q4, "cast2": cast2, "y_t2": y_t2, "e_t": e_t,
            "e_c": e_c, "e_q": e_q, "sig": sig, "m1": m1, "d": d, "d_q": d_q, "x_i": x_i, "x_q": x_q, "m2": m2,
            "y": y, "cast": cast, "y_t": y_t, "y_c": y_c, "y_q": y_q, "store_y": store_y,
            "store_codes": store_codes, "store_scales": store_scales,
        }
        for step in plan():
            steps[step[0]](*step[1:])
